import numpy as np, ml_dtypes
CORES = [30,158,46,174,86,214]
N = 6
def setup_inputs(rng):
    dy = rng.standard_normal((N, 128, N * 128), dtype=np.float32).astype(ml_dtypes.bfloat16)
    dyt = np.concatenate([dy[:, :, 128 * j:128 * j + 128].transpose(0, 2, 1) for j in range(N)], axis=2)
    return {"x": rng.standard_normal((N, 128, 128), dtype=np.float32).astype(ml_dtypes.bfloat16), "wt": rng.standard_normal((N, 128, 128), dtype=np.float32).astype(ml_dtypes.bfloat16), "dy": dy, "dyt": dyt}
def setup_inputs_big(rng):
    d = setup_inputs(rng)
    for k in ("x", "wt", "dy", "dyt"): d[k] = (d[k].astype(np.float32) * 1024.0).astype(d[k].dtype)
    return d
def setup_inputs_small(rng):
    d = setup_inputs(rng)
    for k in ("x", "wt", "dy", "dyt"): d[k] = (d[k].astype(np.float32) * (1 / 1024.0)).astype(d[k].dtype)
    return d
def setup_inputs_apart(rng):
    d = setup_inputs(rng)
    f = (10.0 ** rng.permutation(np.linspace(-1.5, 1.5, N))).astype(np.float32).reshape(N, 1, 1)
    for k in ("x", "wt", "dy", "dyt"): d[k] = (d[k].astype(np.float32) * f).astype(d[k].dtype)
    return d
def tie_inputs(x):
    x = dict(x)
    x["dyt"] = np.concatenate([x["dy"][:, :, 128 * j:128 * j + 128].transpose(0, 2, 1) for j in range(N)], axis=2)
    return x
def reference(x, wt, dy, dyt):
    X, WT, DY, DYT = x.astype(np.float64), wt.astype(np.float64), dy.astype(np.float64), dyt.astype(np.float64)
    dx = np.zeros((N, 128, 128)); dw = np.zeros((N, 128, 128))
    for r in range(N):
        for j in range(N):
            dx[r] += WT[j].T @ DY[j][:, 128 * r:128 * r + 128]
            dw[r] += X[j].T @ DYT[r][:, 128 * j:128 * j + 128]
    return {"dx": dx.astype(ml_dtypes.bfloat16 if x.dtype != np.float64 else np.float64), "dw": dw.astype(ml_dtypes.bfloat16 if x.dtype != np.float64 else np.float64)}

@@ -1,0 +1,128 @@
+from concourse.bass import DstId, RemoteDMATransfer
+from concourse.mybir import AluOpType
+
+N = 6
+B = 128
+
+P_POS = {1: 0, 2: 2, 3: 3, 4: 5, 5: 6}
+WIN = {1: 0, 2: 1, 3: 3, 4: 4, 5: 6}
+X_HBM, X_A, X_B = 7, 1, 4
+ORDER = (5, 1, 2, 3, 4)
+
+SCRATCH = {
+    "wt_sb": ("sbuf", [128, B], "bfloat16"),
+    "dy_sb": ("sbuf", [128, N * B], "bfloat16"),
+    "dyt_sb": ("sbuf", [128, N * B], "bfloat16"),
+    "ob": ("sbuf", [128, 8 * B], "bfloat16"),
+    "land": ("sbuf", [128, 5 * 2 * B], "bfloat16"),
+    "dx_sb": ("sbuf", [128, B], "bfloat16"),
+    "dw_sb": ("sbuf", [128, B], "bfloat16"),
+    "ps_s": ("psum", [128, 512], "float32"),
+    "ps_a": ("psum", [128, 512], "float32"),
+    "ps_b": ("psum", [128, 512], "float32"),
+    "ps_dx": ("psum", [128, 512], "float32"),
+    "ps_dw": ("psum", [128, 512], "float32"),
+}
+SEMAPHORES = ["s_first", "s_x", "s_dyr", "s_dyt", "s_dxo", "s_dwo",
+              "pe_s", "pe_a", "pe_b", "pe_dx", "pe_dw",
+              "v_p5", "v_a", "v_b", "v_acc", "v_dx", "v_dw",
+              "a1", "a2", "a3", "a4", "a5", "ls"]
+
+
+def blk(t, i, n=1):
+    return t[:, i * B:(i + n) * B]
+
+
+def rank_program(g, core, T, topo):
+    r = T.rank_of(core)
+    if r is None:
+        return
+    S = T.sem
+    pe, ve, sy, sc = g.tensor, g.vector, g.sync, g.scalar
+    peer = {k: (r + k) % N for k in range(1, N)}
+    sender = {k: (r - k) % N for k in range(1, N)}
+
+    m = topo.mask(core, T.cores[peer[1]])
+    for k in peer:
+        m &= topo.mask(core, T.cores[peer[k]])
+    eng = [1 << i for i in range(m.bit_length()) if (m >> i) & 1]
+    half = len(eng) // 2
+    m_all, m_lo, m_hi = sum(eng), sum(eng[:half]), sum(eng[half:])
+    n_eng = {5: len(eng), 1: half, 2: half, 3: half, 4: half}
+    arr = {k: S["a%d" % k] for k in peer}
+
+    d5 = peer[5]
+    runs = [(a, b) for (a, b) in ((0, d5), (d5 + 1, N)) if b > a]
+    sy.dma_start(T.wt_sb[:], T.wt[:]).then_inc(S.s_first, 16)
+    sc.dma_start(blk(T.dy_sb, d5), blk(T.dy, d5)).then_inc(S.s_first, 16)
+    sc.dma_start(blk(T.ob, X_HBM), T.x[:]).then_inc(S.s_x, 16)
+    for q, (a, b) in zip((sy, sc), runs):
+        q.dma_start(blk(T.dy_sb, a, b - a), blk(T.dy, a, b - a)).then_inc(S.s_dyr, 16)
+    sy.dma_start(T.dyt_sb[:], T.dyt[:]).then_inc(S.s_dyt, 16)
+
+    def partials(ps, ks, sem):
+        d = [peer[k] for k in ks]
+        if len(d) == 2 and d[1] == d[0] + 1:
+            pe.matmul(ps[:, 0:2 * B], T.wt_sb[:], blk(T.dy_sb, d[0], 2), True, True).then_inc(sem, 1)
+            return 1
+        for i, di in enumerate(d):
+            pe.matmul(blk(ps, i), T.wt_sb[:], blk(T.dy_sb, di), True, True).then_inc(sem, 1)
+        return len(d)
+
+    pe.wait_ge(S.s_first, 32)
+    partials(T.ps_s, (5,), S.pe_s)
+    pe.wait_ge(S.s_dyr, 16 * len(runs))
+    n_a = partials(T.ps_a, (1, 2), S.pe_a)
+    n_b = partials(T.ps_b, (3, 4), S.pe_b)
+    pe.matmul(blk(T.ps_dx, 0), T.wt_sb[:], blk(T.dy_sb, r), True, True).then_inc(S.pe_dx, 1)
+    pe.wait_ge(S.s_x, 16)
+    pe.wait_ge(S.s_dyt, 16)
+    pe.matmul(blk(T.ps_dw, 0), blk(T.ob, X_HBM), blk(T.dyt_sb, r), True, False)
+    for k in ORDER:
+        x_at = 2 * (k - 1) + (1 if P_POS[k] == WIN[k] else 0)
+        pe.wait_ge(arr[k], n_eng[k])
+        mm = pe.matmul(blk(T.ps_dw, 0), blk(T.land, x_at), blk(T.dyt_sb, sender[k]), False, k == ORDER[-1])
+    mm.then_inc(S.pe_dw, 1)
+
+    ve.wait_ge(S.pe_s, 1)
+    ve.tensor_copy(blk(T.ob, P_POS[5]), blk(T.ps_s, 0)).then_inc(S.v_p5, 1)
+    ve.wait_ge(S.s_x, 16)
+    for xc, ps, ks, n_mm, pe_sem, v_sem in ((X_A, T.ps_a, (1, 2), n_a, S.pe_a, S.v_a),
+                                            (X_B, T.ps_b, (3, 4), n_b, S.pe_b, S.v_b)):
+        ve.tensor_copy(blk(T.ob, xc), blk(T.ob, X_HBM)).then_inc(v_sem, 1)
+        ve.wait_ge(pe_sem, n_mm)
+        for i, k in enumerate(ks):
+            ve.tensor_copy(blk(T.ob, P_POS[k]), blk(ps, i)).then_inc(v_sem, 1)
+    ve.wait_ge(S.pe_dx, 1)
+    for i, k in enumerate(ORDER):
+        p_at = 2 * (k - 1) + (0 if P_POS[k] == WIN[k] else 1)
+        ve.wait_ge(arr[k], n_eng[k])
+        if i:
+            ve.wait_ge(S.v_acc, i)
+        if k == ORDER[-1]:
+            ve.tensor_tensor(T.dx_sb[:], blk(T.ps_dx, 0), blk(T.land, p_at), AluOpType.add).then_inc(S.v_dx, 1)
+        else:
+            ve.tensor_tensor(blk(T.ps_dx, 0), blk(T.ps_dx, 0), blk(T.land, p_at), AluOpType.add).then_inc(S.v_acc, 1)
+    ve.wait_ge(S.pe_dw, 1)
+    ve.tensor_copy(T.dw_sb[:], blk(T.ps_dw, 0)).then_inc(S.v_dw, 1)
+
+    def transfer(k, mask):
+        rid, pid = topo.addr(T.cores[peer[k]], core)
+        return RemoteDMATransfer(dst_ids=[DstId(rid=rid, pnc=pid)], dma_engine_mask=mask, remote_sem=arr[k],
+                                 src=blk(T.ob, WIN[k], 2), dst=blk(T.land, 2 * (k - 1), 2))
+
+    g.wait_ge(S.v_p5, 1)
+    g.wait_ge(S.s_x, 16)
+    g.remote_dma_fused([transfer(5, m_all)], local_sem=S.ls)
+    g.wait_ge(S.v_a, 3)
+    g.remote_dma_fused([transfer(1, m_lo), transfer(2, m_hi)], local_sem=S.ls)
+    g.wait_ge(S.v_b, 3)
+    g.remote_dma_fused([transfer(3, m_lo), transfer(4, m_hi)], local_sem=S.ls)
+    g.wait_ge(S.ls, 3 * len(eng))
+
+    sy.wait_ge(S.v_dx, 1)
+    sy.dma_start(T.dx[:], T.dx_sb[:]).then_inc(S.s_dxo, 16)
+    sy.wait_ge(S.s_dxo, 16)
+    sc.wait_ge(S.v_dw, 1)
+    sc.dma_start(T.dw[:], T.dw_sb[:]).then_inc(S.s_dwo, 16)
+    sc.wait_ge(S.s_dwo, 16)

@@ -5,32 +5,42 @@ N = 6
 B = 128
 
 P_POS = {1: 0, 2: 2, 3: 3, 4: 5, 5: 6}
-WIN = {1: 0, 2: 1, 3: 3, 4: 4, 5: 6}
-X_HBM, X_A, X_B = 7, 1, 4
-ORDER = (5, 1, 2, 3, 4)
+WIN = {1: 0, 2: 1, 3: 3, 4: 4}
+X_HBM, X_B = 1, 4
+LAND_X = {k: 2 * (k - 1) + (1 if P_POS[k] == WIN[k] else 0) for k in WIN}
+LAND_P = {k: 2 * (k - 1) + (0 if P_POS[k] == WIN[k] else 1) for k in WIN}
+LAND_X[5], LAND_P[5] = 8, 9
 
 SCRATCH = {
     "wt_sb": ("sbuf", [128, B], "bfloat16"),
     "dy_sb": ("sbuf", [128, N * B], "bfloat16"),
     "dyt_sb": ("sbuf", [128, N * B], "bfloat16"),
-    "ob": ("sbuf", [128, 8 * B], "bfloat16"),
-    "land": ("sbuf", [128, 5 * 2 * B], "bfloat16"),
+    "ob": ("sbuf", [128, 7 * B], "bfloat16"),
+    "land": ("sbuf", [128, 10 * B], "bfloat16"),
     "dx_sb": ("sbuf", [128, B], "bfloat16"),
     "dw_sb": ("sbuf", [128, B], "bfloat16"),
-    "ps_s": ("psum", [128, 512], "float32"),
     "ps_a": ("psum", [128, 512], "float32"),
     "ps_b": ("psum", [128, 512], "float32"),
-    "ps_dx": ("psum", [128, 512], "float32"),
     "ps_dw": ("psum", [128, 512], "float32"),
 }
-SEMAPHORES = ["s_first", "s_x", "s_dyr", "s_dyt", "s_dxo", "s_dwo",
-              "pe_s", "pe_a", "pe_b", "pe_dx", "pe_dw",
-              "v_p5", "v_a", "v_b", "v_acc", "v_dx", "v_dw",
-              "a1", "a2", "a3", "a4", "a5", "ls"]
+SEMAPHORES = ["s_x", "s_a", "s_b", "s_dyt", "s_dxo", "s_dwo",
+              "pe_a", "pe_b", "pe_dw",
+              "v_a", "v_b", "v_p5", "v_acc", "v_dx", "v_dw",
+              "a1", "a2", "a3", "a4", "a5x", "a5p", "ls"]
 
 
 def blk(t, i, n=1):
     return t[:, i * B:(i + n) * B]
+
+
+def runs_of(blocks):
+    out = []
+    for i, b in enumerate(blocks):
+        if out and b == out[-1][1] + out[-1][2]:
+            out[-1][2] += 1
+        else:
+            out.append([i, b, 1])
+    return out
 
 
 def rank_program(g, core, T, topo):
@@ -48,77 +58,70 @@ def rank_program(g, core, T, topo):
     eng = [1 << i for i in range(m.bit_length()) if (m >> i) & 1]
     half = len(eng) // 2
     m_all, m_lo, m_hi = sum(eng), sum(eng[:half]), sum(eng[half:])
-    n_eng = {5: len(eng), 1: half, 2: half, 3: half, 4: half}
-    arr = {k: S["a%d" % k] for k in peer}
+    arr = {k: S["a%d" % k] for k in WIN}
 
-    d5 = peer[5]
-    runs = [(a, b) for (a, b) in ((0, d5), (d5 + 1, N)) if b > a]
-    sy.dma_start(T.wt_sb[:], T.wt[:]).then_inc(S.s_first, 16)
-    sc.dma_start(blk(T.dy_sb, d5), blk(T.dy, d5)).then_inc(S.s_first, 16)
-    sc.dma_start(blk(T.ob, X_HBM), T.x[:]).then_inc(S.s_x, 16)
-    for q, (a, b) in zip((sy, sc), runs):
-        q.dma_start(blk(T.dy_sb, a, b - a), blk(T.dy, a, b - a)).then_inc(S.s_dyr, 16)
-    sy.dma_start(T.dyt_sb[:], T.dyt[:]).then_inc(S.s_dyt, 16)
+    runs_a = runs_of([peer[1], peer[2]])
+    runs_b = runs_of([peer[3], peer[4], peer[5], r])
+    loads = [(blk(T.ob, X_HBM), T.x[:], S.s_x), (T.wt_sb[:], T.wt[:], S.s_a)]
+    loads += [(blk(T.dy_sb, b, n), blk(T.dy, b, n), S.s_a) for _, b, n in runs_a]
+    loads += [(blk(T.dy_sb, b, n), blk(T.dy, b, n), S.s_b) for _, b, n in runs_b]
+    loads += [(T.dyt_sb[:], T.dyt[:], S.s_dyt)]
+    for i, (out, in_, sem) in enumerate(loads):
+        (sy, sc)[i % 2].dma_start(out, in_).then_inc(sem, 16)
 
-    def partials(ps, ks, sem):
-        d = [peer[k] for k in ks]
-        if len(d) == 2 and d[1] == d[0] + 1:
-            pe.matmul(ps[:, 0:2 * B], T.wt_sb[:], blk(T.dy_sb, d[0], 2), True, True).then_inc(sem, 1)
-            return 1
-        for i, di in enumerate(d):
-            pe.matmul(blk(ps, i), T.wt_sb[:], blk(T.dy_sb, di), True, True).then_inc(sem, 1)
-        return len(d)
-
-    pe.wait_ge(S.s_first, 32)
-    partials(T.ps_s, (5,), S.pe_s)
-    pe.wait_ge(S.s_dyr, 16 * len(runs))
-    n_a = partials(T.ps_a, (1, 2), S.pe_a)
-    n_b = partials(T.ps_b, (3, 4), S.pe_b)
-    pe.matmul(blk(T.ps_dx, 0), T.wt_sb[:], blk(T.dy_sb, r), True, True).then_inc(S.pe_dx, 1)
+    pe.wait_ge(S.s_a, 16 * (1 + len(runs_a)))
+    for i, b, n in runs_a:
+        pe.matmul(blk(T.ps_a, i, n), T.wt_sb[:], blk(T.dy_sb, b, n), True, True).then_inc(S.pe_a, 1)
+    pe.wait_ge(S.s_b, 16 * len(runs_b))
+    for i, b, n in runs_b:
+        pe.matmul(blk(T.ps_b, i, n), T.wt_sb[:], blk(T.dy_sb, b, n), True, True).then_inc(S.pe_b, 1)
     pe.wait_ge(S.s_x, 16)
     pe.wait_ge(S.s_dyt, 16)
     pe.matmul(blk(T.ps_dw, 0), blk(T.ob, X_HBM), blk(T.dyt_sb, r), True, False)
-    for k in ORDER:
-        x_at = 2 * (k - 1) + (1 if P_POS[k] == WIN[k] else 0)
-        pe.wait_ge(arr[k], n_eng[k])
-        mm = pe.matmul(blk(T.ps_dw, 0), blk(T.land, x_at), blk(T.dyt_sb, sender[k]), False, k == ORDER[-1])
+    pe.wait_ge(S.a5x, len(eng))
+    pe.matmul(blk(T.ps_dw, 0), blk(T.land, LAND_X[5]), blk(T.dyt_sb, sender[5]), False, False)
+    for k in (1, 2, 3, 4):
+        pe.wait_ge(arr[k], half)
+        mm = pe.matmul(blk(T.ps_dw, 0), blk(T.land, LAND_X[k]), blk(T.dyt_sb, sender[k]), False, k == 4)
     mm.then_inc(S.pe_dw, 1)
 
-    ve.wait_ge(S.pe_s, 1)
-    ve.tensor_copy(blk(T.ob, P_POS[5]), blk(T.ps_s, 0)).then_inc(S.v_p5, 1)
+    acc = blk(T.ps_b, 3)
     ve.wait_ge(S.s_x, 16)
-    for xc, ps, ks, n_mm, pe_sem, v_sem in ((X_A, T.ps_a, (1, 2), n_a, S.pe_a, S.v_a),
-                                            (X_B, T.ps_b, (3, 4), n_b, S.pe_b, S.v_b)):
-        ve.tensor_copy(blk(T.ob, xc), blk(T.ob, X_HBM)).then_inc(v_sem, 1)
-        ve.wait_ge(pe_sem, n_mm)
-        for i, k in enumerate(ks):
-            ve.tensor_copy(blk(T.ob, P_POS[k]), blk(ps, i)).then_inc(v_sem, 1)
-    ve.wait_ge(S.pe_dx, 1)
-    for i, k in enumerate(ORDER):
-        p_at = 2 * (k - 1) + (0 if P_POS[k] == WIN[k] else 1)
-        ve.wait_ge(arr[k], n_eng[k])
+    ve.tensor_copy(blk(T.ob, X_B), blk(T.ob, X_HBM)).then_inc(S.v_b, 1)
+    ve.wait_ge(S.pe_a, len(runs_a))
+    ve.tensor_copy(blk(T.ob, P_POS[1]), blk(T.ps_a, 0)).then_inc(S.v_a, 1)
+    ve.tensor_copy(blk(T.ob, P_POS[2]), blk(T.ps_a, 1)).then_inc(S.v_a, 1)
+    ve.wait_ge(S.pe_b, len(runs_b))
+    ve.tensor_copy(blk(T.ob, P_POS[3]), blk(T.ps_b, 0)).then_inc(S.v_b, 1)
+    ve.tensor_copy(blk(T.ob, P_POS[4]), blk(T.ps_b, 1)).then_inc(S.v_b, 1)
+    ve.tensor_copy(blk(T.ob, P_POS[5]), blk(T.ps_b, 2)).then_inc(S.v_p5, 1)
+    for i, k in enumerate((1, 2, 3, 4)):
+        ve.wait_ge(arr[k], half)
         if i:
             ve.wait_ge(S.v_acc, i)
-        if k == ORDER[-1]:
-            ve.tensor_tensor(T.dx_sb[:], blk(T.ps_dx, 0), blk(T.land, p_at), AluOpType.add).then_inc(S.v_dx, 1)
-        else:
-            ve.tensor_tensor(blk(T.ps_dx, 0), blk(T.ps_dx, 0), blk(T.land, p_at), AluOpType.add).then_inc(S.v_acc, 1)
+        ve.tensor_tensor(acc, acc, blk(T.land, LAND_P[k]), AluOpType.add).then_inc(S.v_acc, 1)
     ve.wait_ge(S.pe_dw, 1)
     ve.tensor_copy(T.dw_sb[:], blk(T.ps_dw, 0)).then_inc(S.v_dw, 1)
+    ve.wait_ge(S.a5p, len(eng))
+    ve.wait_ge(S.v_acc, 4)
+    ve.tensor_tensor(T.dx_sb[:], acc, blk(T.land, LAND_P[5]), AluOpType.add).then_inc(S.v_dx, 1)
 
-    def transfer(k, mask):
+    def transfer(k, mask, src, dst, sem):
         rid, pid = topo.addr(T.cores[peer[k]], core)
-        return RemoteDMATransfer(dst_ids=[DstId(rid=rid, pnc=pid)], dma_engine_mask=mask, remote_sem=arr[k],
-                                 src=blk(T.ob, WIN[k], 2), dst=blk(T.land, 2 * (k - 1), 2))
+        return RemoteDMATransfer(dst_ids=[DstId(rid=rid, pnc=pid)], dma_engine_mask=mask, remote_sem=sem, src=src, dst=dst)
 
-    g.wait_ge(S.v_p5, 1)
+    def window(k, mask):
+        return transfer(k, mask, blk(T.ob, WIN[k], 2), blk(T.land, 2 * (k - 1), 2), arr[k])
+
     g.wait_ge(S.s_x, 16)
-    g.remote_dma_fused([transfer(5, m_all)], local_sem=S.ls)
-    g.wait_ge(S.v_a, 3)
-    g.remote_dma_fused([transfer(1, m_lo), transfer(2, m_hi)], local_sem=S.ls)
+    g.remote_dma_fused([transfer(5, m_all, blk(T.ob, X_HBM), blk(T.land, LAND_X[5]), S.a5x)], local_sem=S.ls)
+    g.wait_ge(S.v_a, 2)
+    g.remote_dma_fused([window(1, m_lo), window(2, m_hi)], local_sem=S.ls)
     g.wait_ge(S.v_b, 3)
-    g.remote_dma_fused([transfer(3, m_lo), transfer(4, m_hi)], local_sem=S.ls)
-    g.wait_ge(S.ls, 3 * len(eng))
+    g.remote_dma_fused([window(3, m_lo), window(4, m_hi)], local_sem=S.ls)
+    g.wait_ge(S.v_p5, 1)
+    g.remote_dma_fused([transfer(5, m_all, blk(T.ob, P_POS[5]), blk(T.land, LAND_P[5]), S.a5p)], local_sem=S.ls)
+    g.wait_ge(S.ls, 4 * len(eng))
 
     sy.wait_ge(S.v_dx, 1)
     sy.dma_start(T.dx[:], T.dx_sb[:]).then_inc(S.s_dxo, 16)

@@ -1,4 +1,3 @@
-from concourse.bass import DstId, RemoteDMATransfer
 from concourse.mybir import AluOpType
 
 N = 6
@@ -12,6 +11,7 @@ LAND_P = {k: 2 * (k - 1) + (0 if P_POS[k] == WIN[k] else 1) for k in WIN}
 LAND_X[5], LAND_P[5] = 8, 9
 
 SCRATCH = {
+    "xd": ("dram", [128, B], "bfloat16"),
     "wt_sb": ("sbuf", [128, B], "bfloat16"),
     "dy_sb": ("sbuf", [128, N * B], "bfloat16"),
     "dyt_sb": ("sbuf", [128, N * B], "bfloat16"),
@@ -19,13 +19,16 @@ SCRATCH = {
     "land": ("sbuf", [128, 10 * B], "bfloat16"),
     "dx_sb": ("sbuf", [128, B], "bfloat16"),
     "dw_sb": ("sbuf", [128, B], "bfloat16"),
-    "ps_a": ("psum", [128, 512], "float32"),
-    "ps_b": ("psum", [128, 512], "float32"),
+    "ps1": ("psum", [128, 512], "float32"),
+    "ps2": ("psum", [128, 512], "float32"),
+    "ps3": ("psum", [128, 512], "float32"),
+    "ps4": ("psum", [128, 512], "float32"),
+    "ps_c": ("psum", [128, 512], "float32"),
     "ps_dw": ("psum", [128, 512], "float32"),
 }
-SEMAPHORES = ["s_x", "s_a", "s_b", "s_dyt", "s_dxo", "s_dwo",
-              "pe_a", "pe_b", "pe_dw",
-              "v_a", "v_b", "v_p5", "v_acc", "v_dx", "v_dw",
+SEMAPHORES = ["s_xd", "s_x", "s_g1", "s_g2", "s_g0", "s_dyt", "s_dxo", "s_dwo",
+              "pe1", "pe2", "pe3", "pe4", "pe_c", "pe_dw",
+              "v1", "v2", "v3", "v4", "v5", "v_acc", "v_dx", "v_dw",
               "a1", "a2", "a3", "a4", "a5x", "a5p", "ls"]
 
 
@@ -35,11 +38,11 @@ def blk(t, i, n=1):
 
 def runs_of(blocks):
     out = []
-    for i, b in enumerate(blocks):
-        if out and b == out[-1][1] + out[-1][2]:
-            out[-1][2] += 1
+    for b in blocks:
+        if out and b == out[-1][0] + out[-1][1]:
+            out[-1][1] += 1
         else:
-            out.append([i, b, 1])
+            out.append([b, 1])
     return out
 
 
@@ -49,79 +52,101 @@ def rank_program(g, core, T, topo):
         return
     S = T.sem
     pe, ve, sy, sc = g.tensor, g.vector, g.sync, g.scalar
-    peer = {k: (r + k) % N for k in range(1, N)}
-    sender = {k: (r - k) % N for k in range(1, N)}
+
+    chips = []
+    for c in T.cores:
+        if topo.chip(c) not in chips:
+            chips.append(topo.chip(c))
+    grp = [[j for j, c in enumerate(T.cores) if topo.chip(c) == ch] for ch in chips]
+    n_g = len(grp)
+    p = chips.index(topo.chip(core))
+    b = grp[p].index(r)
+    g1, g2 = grp[(p + 1) % n_g], grp[(p + 2) % n_g]
+    peer = {1: g1[b], 2: g1[1 - b], 3: g2[b], 4: g2[1 - b], 5: grp[p][1 - b]}
+    sender = {1: g2[b], 2: g2[1 - b], 3: g1[b], 4: g1[1 - b], 5: grp[p][1 - b]}
 
     m = topo.mask(core, T.cores[peer[1]])
     for k in peer:
         m &= topo.mask(core, T.cores[peer[k]])
-    eng = [1 << i for i in range(m.bit_length()) if (m >> i) & 1]
-    half = len(eng) // 2
-    m_all, m_lo, m_hi = sum(eng), sum(eng[:half]), sum(eng[half:])
+    n_e = sum((m >> i) & 1 for i in range(m.bit_length()))
     arr = {k: S["a%d" % k] for k in WIN}
 
-    runs_a = runs_of([peer[1], peer[2]])
-    runs_b = runs_of([peer[3], peer[4], peer[5], r])
-    loads = [(blk(T.ob, X_HBM), T.x[:], S.s_x), (T.wt_sb[:], T.wt[:], S.s_a)]
-    loads += [(blk(T.dy_sb, b, n), blk(T.dy, b, n), S.s_a) for _, b, n in runs_a]
-    loads += [(blk(T.dy_sb, b, n), blk(T.dy, b, n), S.s_b) for _, b, n in runs_b]
-    loads += [(T.dyt_sb[:], T.dyt[:], S.s_dyt)]
+    def dy_loads(ranks, sem):
+        return [(blk(T.dy_sb, a, n), blk(T.dy, a, n), sem) for a, n in runs_of(sorted(ranks))]
+
+    l1, l2, l0 = dy_loads(g1, S.s_g1), dy_loads(g2, S.s_g2), dy_loads(grp[p], S.s_g0)
+    loads = [(T.xd[:], T.x[:], S.s_xd), (T.wt_sb[:], T.wt[:], S.s_g1)] + l1
+    loads += [(blk(T.ob, X_HBM), T.x[:], S.s_x)] + l2 + l0 + [(T.dyt_sb[:], T.dyt[:], S.s_dyt)]
     for i, (out, in_, sem) in enumerate(loads):
         (sy, sc)[i % 2].dma_start(out, in_).then_inc(sem, 16)
 
-    pe.wait_ge(S.s_a, 16 * (1 + len(runs_a)))
-    for i, b, n in runs_a:
-        pe.matmul(blk(T.ps_a, i, n), T.wt_sb[:], blk(T.dy_sb, b, n), True, True).then_inc(S.pe_a, 1)
-    pe.wait_ge(S.s_b, 16 * len(runs_b))
-    for i, b, n in runs_b:
-        pe.matmul(blk(T.ps_b, i, n), T.wt_sb[:], blk(T.dy_sb, b, n), True, True).then_inc(S.pe_b, 1)
+    def partial(ps, i, rank, sem):
+        pe.matmul(blk(ps, i), T.wt_sb[:], blk(T.dy_sb, rank), True, True).then_inc(sem, 1)
+
+    pe.wait_ge(S.s_g1, 16 * (1 + len(l1)))
+    partial(T.ps1, 0, peer[1], S.pe1)
+    partial(T.ps2, 0, peer[2], S.pe2)
+    pe.wait_ge(S.s_g2, 16 * len(l2))
+    partial(T.ps3, 0, peer[3], S.pe3)
+    partial(T.ps4, 0, peer[4], S.pe4)
+    pe.wait_ge(S.s_g0, 16 * len(l0))
+    partial(T.ps_c, 1, peer[5], S.pe_c)
+    partial(T.ps_c, 0, r, S.pe_c)
     pe.wait_ge(S.s_x, 16)
     pe.wait_ge(S.s_dyt, 16)
     pe.matmul(blk(T.ps_dw, 0), blk(T.ob, X_HBM), blk(T.dyt_sb, r), True, False)
-    pe.wait_ge(S.a5x, len(eng))
+    pe.wait_ge(S.a5x, n_e)
     pe.matmul(blk(T.ps_dw, 0), blk(T.land, LAND_X[5]), blk(T.dyt_sb, sender[5]), False, False)
     for k in (1, 2, 3, 4):
-        pe.wait_ge(arr[k], half)
+        pe.wait_ge(arr[k], n_e)
         mm = pe.matmul(blk(T.ps_dw, 0), blk(T.land, LAND_X[k]), blk(T.dyt_sb, sender[k]), False, k == 4)
     mm.then_inc(S.pe_dw, 1)
 
-    acc = blk(T.ps_b, 3)
+    ve.wait_ge(S.pe1, 1)
+    ve.tensor_copy(blk(T.ob, P_POS[1]), blk(T.ps1, 0)).then_inc(S.v1, 1)
+    ve.wait_ge(S.pe2, 1)
+    ve.tensor_copy(blk(T.ob, P_POS[2]), blk(T.ps2, 0)).then_inc(S.v2, 1)
     ve.wait_ge(S.s_x, 16)
-    ve.tensor_copy(blk(T.ob, X_B), blk(T.ob, X_HBM)).then_inc(S.v_b, 1)
-    ve.wait_ge(S.pe_a, len(runs_a))
-    ve.tensor_copy(blk(T.ob, P_POS[1]), blk(T.ps_a, 0)).then_inc(S.v_a, 1)
-    ve.tensor_copy(blk(T.ob, P_POS[2]), blk(T.ps_a, 1)).then_inc(S.v_a, 1)
-    ve.wait_ge(S.pe_b, len(runs_b))
-    ve.tensor_copy(blk(T.ob, P_POS[3]), blk(T.ps_b, 0)).then_inc(S.v_b, 1)
-    ve.tensor_copy(blk(T.ob, P_POS[4]), blk(T.ps_b, 1)).then_inc(S.v_b, 1)
-    ve.tensor_copy(blk(T.ob, P_POS[5]), blk(T.ps_b, 2)).then_inc(S.v_p5, 1)
+    ve.tensor_copy(blk(T.ob, X_B), blk(T.ob, X_HBM)).then_inc(S.v3, 1)
+    ve.wait_ge(S.pe3, 1)
+    ve.tensor_copy(blk(T.ob, P_POS[3]), blk(T.ps3, 0)).then_inc(S.v3, 1)
+    ve.wait_ge(S.pe4, 1)
+    ve.tensor_copy(blk(T.ob, P_POS[4]), blk(T.ps4, 0)).then_inc(S.v4, 1)
+    ve.wait_ge(S.pe_c, 2)
+    ve.tensor_copy(blk(T.ob, P_POS[5]), blk(T.ps_c, 1)).then_inc(S.v5, 1)
+    acc = blk(T.ps_c, 0)
     for i, k in enumerate((1, 2, 3, 4)):
-        ve.wait_ge(arr[k], half)
+        ve.wait_ge(arr[k], n_e)
         if i:
             ve.wait_ge(S.v_acc, i)
         ve.tensor_tensor(acc, acc, blk(T.land, LAND_P[k]), AluOpType.add).then_inc(S.v_acc, 1)
     ve.wait_ge(S.pe_dw, 1)
     ve.tensor_copy(T.dw_sb[:], blk(T.ps_dw, 0)).then_inc(S.v_dw, 1)
-    ve.wait_ge(S.a5p, len(eng))
+    ve.wait_ge(S.a5p, n_e)
     ve.wait_ge(S.v_acc, 4)
     ve.tensor_tensor(T.dx_sb[:], acc, blk(T.land, LAND_P[5]), AluOpType.add).then_inc(S.v_dx, 1)
 
-    def transfer(k, mask, src, dst, sem):
+    def send(k, src, dst, sem):
         rid, pid = topo.addr(T.cores[peer[k]], core)
-        return RemoteDMATransfer(dst_ids=[DstId(rid=rid, pnc=pid)], dma_engine_mask=mask, remote_sem=sem, src=src, dst=dst)
+        g.remote_dma(out_ap=dst, in_ap=src, remote_sem=sem, local_sem=S.ls, pid=pid, routing_id=rid, dma_engine_mask=m)
 
-    def window(k, mask):
-        return transfer(k, mask, blk(T.ob, WIN[k], 2), blk(T.land, 2 * (k - 1), 2), arr[k])
+    def window(k):
+        send(k, blk(T.ob, WIN[k], 2), blk(T.land, 2 * (k - 1), 2), arr[k])
 
+    g.wait_ge(S.s_xd, 16)
+    send(5, T.xd[:], blk(T.land, LAND_X[5]), S.a5x)
     g.wait_ge(S.s_x, 16)
-    g.remote_dma_fused([transfer(5, m_all, blk(T.ob, X_HBM), blk(T.land, LAND_X[5]), S.a5x)], local_sem=S.ls)
-    g.wait_ge(S.v_a, 2)
-    g.remote_dma_fused([window(1, m_lo), window(2, m_hi)], local_sem=S.ls)
-    g.wait_ge(S.v_b, 3)
-    g.remote_dma_fused([window(3, m_lo), window(4, m_hi)], local_sem=S.ls)
-    g.wait_ge(S.v_p5, 1)
-    g.remote_dma_fused([transfer(5, m_all, blk(T.ob, P_POS[5]), blk(T.land, LAND_P[5]), S.a5p)], local_sem=S.ls)
-    g.wait_ge(S.ls, 4 * len(eng))
+    g.wait_ge(S.v1, 1)
+    window(1)
+    g.wait_ge(S.v2, 1)
+    window(2)
+    g.wait_ge(S.v3, 2)
+    window(3)
+    g.wait_ge(S.v4, 1)
+    window(4)
+    g.wait_ge(S.v5, 1)
+    send(5, blk(T.ob, P_POS[5]), blk(T.land, LAND_P[5]), S.a5p)
+    g.wait_ge(S.ls, 6 * n_e)
 
     sy.wait_ge(S.v_dx, 1)
     sy.dma_start(T.dx[:], T.dx_sb[:]).then_inc(S.s_dxo, 16)

from concourse.mybir import AluOpType

N = 6
B = 128

P_POS = {1: 0, 2: 2, 3: 3, 4: 5, 5: 6}
WIN = {1: 0, 2: 1, 3: 3, 4: 4}
X_HBM, X_B = 1, 4
LAND_X = {k: 2 * (k - 1) + (1 if P_POS[k] == WIN[k] else 0) for k in WIN}
LAND_P = {k: 2 * (k - 1) + (0 if P_POS[k] == WIN[k] else 1) for k in WIN}
LAND_X[5], LAND_P[5] = 8, 9

SCRATCH = {
    "xd": ("dram", [128, B], "bfloat16"),
    "wt_sb": ("sbuf", [128, B], "bfloat16"),
    "dy_sb": ("sbuf", [128, N * B], "bfloat16"),
    "dyt_sb": ("sbuf", [128, N * B], "bfloat16"),
    "ob": ("sbuf", [128, 7 * B], "bfloat16"),
    "land": ("sbuf", [128, 10 * B], "bfloat16"),
    "dx_sb": ("sbuf", [128, B], "bfloat16"),
    "dw_sb": ("sbuf", [128, B], "bfloat16"),
    "ps1": ("psum", [128, 512], "float32"),
    "ps2": ("psum", [128, 512], "float32"),
    "ps3": ("psum", [128, 512], "float32"),
    "ps4": ("psum", [128, 512], "float32"),
    "ps_c": ("psum", [128, 512], "float32"),
    "ps_dw": ("psum", [128, 512], "float32"),
}
SEMAPHORES = ["s_xd", "s_x", "s_g1", "s_g2", "s_g0", "s_dyt", "s_dxo", "s_dwo",
              "pe1", "pe2", "pe3", "pe4", "pe_c", "pe_dw",
              "v1", "v2", "v3", "v4", "v5", "v_acc", "v_dx", "v_dw",
              "a1", "a2", "a3", "a4", "a5x", "a5p", "ls"]


def blk(t, i, n=1):
    return t[:, i * B:(i + n) * B]


def runs_of(blocks):
    out = []
    for b in blocks:
        if out and b == out[-1][0] + out[-1][1]:
            out[-1][1] += 1
        else:
            out.append([b, 1])
    return out


def rank_program(g, core, T, topo):
    r = T.rank_of(core)
    if r is None:
        return
    S = T.sem
    pe, ve, sy, sc = g.tensor, g.vector, g.sync, g.scalar

    chips = []
    for c in T.cores:
        if topo.chip(c) not in chips:
            chips.append(topo.chip(c))
    grp = [[j for j, c in enumerate(T.cores) if topo.chip(c) == ch] for ch in chips]
    n_g = len(grp)
    p = chips.index(topo.chip(core))
    b = grp[p].index(r)
    g1, g2 = grp[(p + 1) % n_g], grp[(p + 2) % n_g]
    peer = {1: g1[b], 2: g1[1 - b], 3: g2[b], 4: g2[1 - b], 5: grp[p][1 - b]}
    sender = {1: g2[b], 2: g2[1 - b], 3: g1[b], 4: g1[1 - b], 5: grp[p][1 - b]}

    m = topo.mask(core, T.cores[peer[1]])
    for k in peer:
        m &= topo.mask(core, T.cores[peer[k]])
    n_e = sum((m >> i) & 1 for i in range(m.bit_length()))
    arr = {k: S["a%d" % k] for k in WIN}

    def dy_loads(ranks, sem):
        return [(blk(T.dy_sb, a, n), blk(T.dy, a, n), sem) for a, n in runs_of(sorted(ranks))]

    l1, l2, l0 = dy_loads(g1, S.s_g1), dy_loads(g2, S.s_g2), dy_loads(grp[p], S.s_g0)
    loads = [(T.xd[:], T.x[:], S.s_xd), (T.wt_sb[:], T.wt[:], S.s_g1)] + l1
    loads += [(blk(T.ob, X_HBM), T.x[:], S.s_x)] + l2 + l0 + [(T.dyt_sb[:], T.dyt[:], S.s_dyt)]
    for i, (out, in_, sem) in enumerate(loads):
        (sy, sc)[i % 2].dma_start(out, in_).then_inc(sem, 16)

    def partial(ps, i, rank, sem):
        pe.matmul(blk(ps, i), T.wt_sb[:], blk(T.dy_sb, rank), True, True).then_inc(sem, 1)

    pe.wait_ge(S.s_g1, 16 * (1 + len(l1)))
    partial(T.ps1, 0, peer[1], S.pe1)
    partial(T.ps2, 0, peer[2], S.pe2)
    pe.wait_ge(S.s_g2, 16 * len(l2))
    partial(T.ps3, 0, peer[3], S.pe3)
    partial(T.ps4, 0, peer[4], S.pe4)
    pe.wait_ge(S.s_g0, 16 * len(l0))
    partial(T.ps_c, 1, peer[5], S.pe_c)
    partial(T.ps_c, 0, r, S.pe_c)
    pe.wait_ge(S.s_x, 16)
    pe.wait_ge(S.s_dyt, 16)
    pe.matmul(blk(T.ps_dw, 0), blk(T.ob, X_HBM), blk(T.dyt_sb, r), True, False)
    pe.wait_ge(S.a5x, n_e)
    pe.matmul(blk(T.ps_dw, 0), blk(T.land, LAND_X[5]), blk(T.dyt_sb, sender[5]), False, False)
    for k in (1, 2, 3, 4):
        pe.wait_ge(arr[k], n_e)
        mm = pe.matmul(blk(T.ps_dw, 0), blk(T.land, LAND_X[k]), blk(T.dyt_sb, sender[k]), False, k == 4)
    mm.then_inc(S.pe_dw, 1)

    ve.wait_ge(S.pe1, 1)
    ve.tensor_copy(blk(T.ob, P_POS[1]), blk(T.ps1, 0)).then_inc(S.v1, 1)
    ve.wait_ge(S.pe2, 1)
    ve.tensor_copy(blk(T.ob, P_POS[2]), blk(T.ps2, 0)).then_inc(S.v2, 1)
    ve.wait_ge(S.s_x, 16)
    ve.tensor_copy(blk(T.ob, X_B), blk(T.ob, X_HBM)).then_inc(S.v3, 1)
    ve.wait_ge(S.pe3, 1)
    ve.tensor_copy(blk(T.ob, P_POS[3]), blk(T.ps3, 0)).then_inc(S.v3, 1)
    ve.wait_ge(S.pe4, 1)
    ve.tensor_copy(blk(T.ob, P_POS[4]), blk(T.ps4, 0)).then_inc(S.v4, 1)
    ve.wait_ge(S.pe_c, 2)
    ve.tensor_copy(blk(T.ob, P_POS[5]), blk(T.ps_c, 1)).then_inc(S.v5, 1)
    acc = blk(T.ps_c, 0)
    for i, k in enumerate((1, 2, 3, 4)):
        ve.wait_ge(arr[k], n_e)
        if i:
            ve.wait_ge(S.v_acc, i)
        ve.tensor_tensor(acc, acc, blk(T.land, LAND_P[k]), AluOpType.add).then_inc(S.v_acc, 1)
    ve.wait_ge(S.pe_dw, 1)
    ve.tensor_copy(T.dw_sb[:], blk(T.ps_dw, 0)).then_inc(S.v_dw, 1)
    ve.wait_ge(S.a5p, n_e)
    ve.wait_ge(S.v_acc, 4)
    ve.tensor_tensor(T.dx_sb[:], acc, blk(T.land, LAND_P[5]), AluOpType.add).then_inc(S.v_dx, 1)

    def send(k, src, dst, sem):
        rid, pid = topo.addr(T.cores[peer[k]], core)
        g.remote_dma(out_ap=dst, in_ap=src, remote_sem=sem, local_sem=S.ls, pid=pid, routing_id=rid, dma_engine_mask=m)

    def window(k):
        send(k, blk(T.ob, WIN[k], 2), blk(T.land, 2 * (k - 1), 2), arr[k])

    g.wait_ge(S.s_xd, 16)
    send(5, T.xd[:], blk(T.land, LAND_X[5]), S.a5x)
    g.wait_ge(S.s_x, 16)
    g.wait_ge(S.v1, 1)
    window(1)
    g.wait_ge(S.v2, 1)
    window(2)
    g.wait_ge(S.v3, 2)
    window(3)
    g.wait_ge(S.v4, 1)
    window(4)
    g.wait_ge(S.v5, 1)
    send(5, blk(T.ob, P_POS[5]), blk(T.land, LAND_P[5]), S.a5p)
    g.wait_ge(S.ls, 6 * n_e)

    sy.wait_ge(S.v_dx, 1)
    sy.dma_start(T.dx[:], T.dx_sb[:]).then_inc(S.s_dxo, 16)
    sy.wait_ge(S.s_dxo, 16)
    sc.wait_ge(S.v_dw, 1)
    sc.dma_start(T.dw[:], T.dw_sb[:]).then_inc(S.s_dwo, 16)
    sc.wait_ge(S.s_dwo, 16)
